import numpy as np
import ml_dtypes


def mxq(x, axis, fmt="e4m3"):
    dtype, down = {"e4m3": (ml_dtypes.float8_e4m3fn, 7), "e5m2": (ml_dtypes.float8_e5m2, 14)}[fmt]
    v = np.moveaxis(np.asarray(x, np.float32).astype(ml_dtypes.bfloat16).astype(np.float64), axis, -1)
    blocks = v.reshape(v.shape[:-1] + (-1, 32))
    amax = np.abs(blocks).max(-1, keepdims=True)
    byte = np.maximum(np.where(amax > 0, np.frexp(amax)[1] - 1 + 127, 0) - down, 1)
    scale = np.exp2(byte - 127.0)
    codes = (blocks / scale).astype(np.float32).astype(dtype).astype(np.float64)
    return np.moveaxis((codes * scale).reshape(v.shape), -1, axis)


WIDE = False


def mx_kscale(k):
    if not WIDE:
        return np.ones(k)
    levels = np.array([10, -10, 5, -5, 0])
    if k % 512:
        return np.exp2(np.random.permutation(np.resize(levels, k // 32))).repeat(32)
    a = np.empty((k // 512, 16))
    for p in range(k // 512):
        a[p, :8] = np.random.permutation(np.resize(levels, 8))
        for g in range(8):
            far = levels[np.abs(levels - a[p, g]) >= 10]
            a[p, g + 8] = far[np.random.randint(len(far))]
    return np.exp2(a.ravel()).repeat(32)


def f64(x):
    return np.asarray(x).astype(np.float64)


def striped8(idx):
    return np.asarray(idx).reshape(8, -1, 16).transpose(0, 2, 1).reshape(128, -1).astype(np.uint16)


def unstriped8(offs):
    return offs.reshape(8, 16, -1).transpose(0, 2, 1).reshape(8, -1).astype(np.int64)


def pick8(x, idx, run):
    r = np.arange(len(x))
    return x[r[:, None], idx[r % (8 * run) // run]]


E2M1 = np.array([0.0, 0.5, 1.0, 1.5, 2.0, 3.0, 4.0, 6.0, -0.0, -0.5, -1.0, -1.5, -2.0, -3.0, -4.0, -6.0])


def pack_weight(w, fmt):
    k, n = w.shape
    w = f64(np.asarray(w, np.float32).astype(ml_dtypes.bfloat16)).reshape(k // 32, 32, n)
    amax = np.abs(w).max(1)
    if fmt == "e4m3":
        byte = np.frexp(amax)[1] - 1 + 127 - 7
    else:
        mant, ex = np.frexp(amax / 6.0)
        byte = np.where(mant > 0.5, ex, ex - 1) + 127
    byte = np.clip(np.where(amax > 0, byte, 1), 1, 254)
    scaled = (w * np.exp2(127.0 - byte)[:, None, :]).reshape(k, n).astype(np.float32)
    by_word = np.ascontiguousarray(scaled.reshape(k // 512, 128, 4, n).transpose(0, 1, 3, 2))
    if fmt == "e4m3":
        words = by_word.astype(ml_dtypes.float8_e4m3fn).view(np.uint8)
    else:
        c = by_word.astype(ml_dtypes.float4_e2m1fn).view(np.uint8) & 0xF
        words = (c[..., 0::2] | (c[..., 1::2] << 4)).reshape(k // 512, 128, 2 * n)
    return np.ascontiguousarray(words), np.ascontiguousarray(byte.astype(np.uint8).reshape(k // 512, 16, n))


def unpack_weight(words, scales, fmt):
    g, _, n = scales.shape
    words = np.ascontiguousarray(words).reshape(g, 128, n, -1)
    if fmt == "e4m3":
        vals = words.view(ml_dtypes.float8_e4m3fn).astype(np.float64)
    else:
        nib = np.empty((g, 128, n, 4), np.uint8)
        nib[..., 0::2] = words & 0xF
        nib[..., 1::2] = words >> 4
        vals = E2M1[nib]
    vals = vals * np.repeat(np.exp2(scales.astype(np.float64) - 127.0), 8, axis=1)[..., None]
    return vals.transpose(0, 1, 3, 2).reshape(g * 512, n)


D, T, I, Q, E = 512, 1024, 512, 512, 256


def setup_inputs():
    n = np.random.standard_normal
    idx = np.stack([np.random.permutation(T)[:I] for _ in range(8)])
    idx2 = np.stack([np.random.permutation(T)[:I] for _ in range(8)])
    idx3 = np.stack([np.random.permutation(T)[:I] for _ in range(8)])
    idx4 = np.stack([np.random.permutation(T)[:I] for _ in range(8)])
    idx5 = np.stack([np.random.permutation(T)[:I] for _ in range(8)])
    idx6 = np.stack([np.random.permutation(T)[:I] for _ in range(8)])
    fd = mx_kscale(D)
    fq = mx_kscale(Q)
    keysp = pack_weight(n((D, T)) / fd[:, None], "e2m1")
    mixp = pack_weight(n((Q, E)) * 1.0 / np.sqrt(Q) / fq[:, None], "e4m3")
    return {
        "query": (n((D, Q)) * 1.0 / np.sqrt(D) * fd[:, None]).astype(np.float32),
        "keys_words": keysp[0],
        "keys_scales": keysp[1],
        "rowf": (np.random.uniform(0.5, 2.0, (Q, 1)) * fq[:, None]).astype(np.float32),
        "mix_words": mixp[0],
        "mix_scales": mixp[1],
        "offs": striped8(idx),
        "offs2": striped8(idx2),
        "offs3": striped8(idx3),
        "offs4": striped8(idx4),
        "offs5": striped8(idx5),
        "offs6": striped8(idx6),
    }


def reference(query, keys_words, keys_scales, rowf, mix_words, mix_scales, offs, offs2, offs3, offs4, offs5, offs6):
    idx = unstriped8(offs)
    idx2 = unstriped8(offs2)
    idx3 = unstriped8(offs3)
    idx4 = unstriped8(offs4)
    idx5 = unstriped8(offs5)
    idx6 = unstriped8(offs6)
    keysu = unpack_weight(keys_words, keys_scales, "e2m1")
    mixu = unpack_weight(mix_words, mix_scales, "e4m3")
    queryq = mxq(f64(query), 0, "e4m3")
    a = queryq.T @ keysu
    f1 = np.zeros((Q, T))
    f1[np.arange(Q)[:, None], idx2[np.arange(Q) % 512 // 64]] = pick8(a, idx, 64)
    c1 = a - f1
    w = np.maximum(pick8(c1, idx3, 64), pick8(a, idx, 64))
    f2 = np.zeros((Q, T))
    f2[np.arange(Q)[:, None], idx4[np.arange(Q) % 512 // 64]] = w
    c2 = c1 + f2
    g = pick8(c2, idx5, 64) - pick8(c1, idx6, 64)
    gw = g * f64(rowf)
    gwq = mxq(gw, 0, "e4m3")
    y = mixu.T @ gwq
    return y

@@ -1,0 +1,245 @@
+from contextlib import ExitStack
+
+import concourse.mybir as mybir
+
+D, T, I, Q, E = 512, 1024, 512, 512, 256
+FLOPS = 2 * D * Q * T + 2 * Q * E * I
+
+F32 = mybir.dt.float32
+BF16 = mybir.dt.bfloat16
+I32 = mybir.dt.int32
+U32 = mybir.dt.uint32
+U16 = mybir.dt.uint16
+U8 = mybir.dt.uint8
+FP8X4 = mybir.dt.float8_e4m3fn_x4
+FP4X4 = mybir.dt.float4_e2m1fn_x4
+ALU = mybir.AluOpType
+COPY = mybir.ActivationFunctionType.Copy
+
+P = 128
+PACK = 4
+BANK = 512
+HALF = I // 2
+LIST_COLS = I // 16
+
+
+def tile_attend_backtrack_one_mixed_kernel(
+    tc, query, keys_words, keys_scales, rowf, mix_words, mix_scales, offs, offs2, offs3, offs4, offs5, offs6, out
+):
+    nc = tc.nc
+    with ExitStack() as ctx:
+        lists = ctx.enter_context(tc.tile_pool(name="lists", bufs=1))
+        keep = ctx.enter_context(tc.tile_pool(name="keep", bufs=1))
+        psum = ctx.enter_context(tc.psum_pool(name="psum", bufs=1))
+
+        def sb(name, shape, dtype, tag=None):
+            return keep.tile(shape, dtype, name=name, tag=tag or name, align_bytes=64)
+
+        idx1 = lists.tile([P, LIST_COLS], U16, name="idx1")
+        idx2 = lists.tile([P, LIST_COLS], U16, name="idx2")
+        idx3 = lists.tile([P, LIST_COLS], U16, name="idx3")
+        idx4 = lists.tile([P, LIST_COLS], U16, name="idx4")
+        idx5 = lists.tile([P, LIST_COLS], U16, name="idx5")
+        idx6 = lists.tile([P, LIST_COLS], U16, name="idx6")
+
+        def half_list(idx, h):
+            return idx[:, h * LIST_COLS // 2 : (h + 1) * LIST_COLS // 2]
+
+        def half(h):
+            return slice(h * HALF, (h + 1) * HALF)
+
+        k_words = sb("k_words", [P, 2 * T], U8)
+        k_scales = sb("k_scales", [P, T], U8)
+        m_words = sb("m_words", [P, E], U32)
+        m_scales = sb("m_scales", [P, E], U8)
+        row_factor = sb("row_factor", [P, PACK], F32)
+        q_raw = [sb("q_raw%d" % h, [P, PACK, Q // 2], F32) for h in range(2)]
+        f1 = [sb("f1_%d" % b, [P, T], F32) for b in range(2)]
+        f2 = [sb("f2_%d" % b, [P, T], F32) for b in range(2)]
+
+        nc.vector.memset(k_scales[:].bitcast(U32), 0)
+        q_rows = query.rearrange("(p j) q -> p j q", j=PACK)
+        nc.sync.dma_start(out=q_raw[0][:], in_=q_rows[:, :, 0 : Q // 2])
+        for g in range(4):
+            nc.sync.dma_start(
+                out=k_scales[32 * g : 32 * g + 4, :].bitcast(I32), in_=keys_scales[0, 4 * g : 4 * g + 4, :].bitcast(I32)
+            )
+        nc.sync.dma_start(out=q_raw[1][:], in_=q_rows[:, :, Q // 2 : Q])
+        nc.sync.dma_start(out=k_words[:].bitcast(I32), in_=keys_words[0].bitcast(I32))
+        nc.sync.dma_start(idx1[:], offs)
+        nc.sync.dma_start(idx2[:], offs2)
+        nc.sync.dma_start(idx3[:], offs3)
+        nc.sync.dma_start(idx6[:], offs6)
+        nc.sync.dma_start(out=row_factor[:], in_=rowf.rearrange("(p r) o -> p (r o)", r=PACK))
+        nc.sync.dma_start(idx4[:], offs4)
+        nc.sync.dma_start(idx5[:], offs5)
+        for window in f1 + f2:
+            nc.vector.memset(window[:], 0.0)
+        nc.vector.memset(m_scales[:].bitcast(U32), 0)
+        nc.sync.dma_start(out=m_words[:].bitcast(I32), in_=mix_words[0].rearrange("p n t -> p (n t)").bitcast(I32))
+        for g in range(4):
+            nc.sync.dma_start(
+                out=m_scales[32 * g : 32 * g + 4, :].bitcast(I32), in_=mix_scales[0, 4 * g : 4 * g + 4, :].bitcast(I32)
+            )
+
+        q_bf = sb("q_bf", [P, PACK, P, PACK], BF16)
+        q_codes = sb("q_codes", [P, Q], U32)
+        q_scales = sb("q_scales", [P, Q], U8)
+        q_flat = q_bf[:].rearrange("p r m j -> p (r m j)")
+
+        def deal_queries(h, r0, r1):
+            nc.vector.tensor_copy(
+                out=q_bf[:, r0:r1, h * P // 2 : (h + 1) * P // 2, :].rearrange("p r m j -> p m j r"),
+                in_=q_raw[h][:].rearrange("p j (m r) -> p m j r", r=PACK)[:, :, :, r0:r1],
+            )
+
+        def quantize_queries(r0, r1):
+            nc.vector.quantize_mx(
+                out=q_codes[:, r0 * P : r1 * P].bitcast(FP8X4),
+                scales=q_scales[:, r0 * P : r1 * P],
+                in_=q_flat[:, r0 * P * PACK : r1 * P * PACK],
+            )
+
+        deal_queries(0, 0, PACK)
+        deal_queries(1, 0, 1)
+        quantize_queries(0, 1)
+
+        a = [sb("a%d" % r, [P, T], F32) for r in range(PACK)]
+        c1 = [sb("c1_%d" % r, [P, T], F32) for r in range(PACK)]
+        c2 = [sb("c2_%d" % r, [P, T], F32) for r in range(PACK)]
+        a_at1 = sb("a_at1", [P, PACK, I], F32)
+        c1_at3 = sb("c1_at3", [P, PACK, I], F32)
+        w = sb("w", [P, PACK, I], F32)
+        c1_at6 = sb("c1_at6", [P, PACK, I], F32)
+        c2_at5 = sb("c2_at5", [P, PACK, I], F32)
+        gw = sb("gw", [P, PACK, I], BF16)
+
+        def gather(dst, window, offsets):
+            nc.scalar.activation(dst, window[:].indirect(offsets), COPY)
+
+        def scores(r, n, width, bank_tag, on_vector):
+            cols = slice(n * width, (n + 1) * width)
+            bank = psum.tile([P, width], F32, name="score_bank", tag=bank_tag)
+            nc.tensor.matmul_mx(
+                out=bank[:],
+                lhsT=q_codes[:, r * P : (r + 1) * P].bitcast(FP8X4),
+                lhsT_scale=q_scales[:, r * P : (r + 1) * P],
+                rhs=k_words[:, 2 * n * width : 2 * (n + 1) * width].bitcast(FP4X4),
+                rhs_scale=k_scales[:, cols],
+                start=True,
+                stop=True,
+            )
+            if on_vector:
+                nc.vector.tensor_copy(out=a[r][:, cols], in_=bank[:])
+            else:
+                nc.scalar.activation(a[r][:, cols], bank[:], COPY)
+
+        for r in range(PACK):
+            if r == 0:
+                for n in range(4):
+                    scores(r, n, T // 4, "bank%d" % n, n % 2 == 0)
+                deal_queries(1, 1, PACK)
+                quantize_queries(1, 2)
+                quantize_queries(2, PACK)
+                for h in range(2):
+                    gather(a_at1[:, r, half(h)], a[r], half_list(idx1, h))
+                    nc.vector.tensor_copy(f1[r % 2][:].indirect(half_list(idx2, h)), a_at1[:, r, half(h)])
+            else:
+                for n in range(2):
+                    scores(r, n, BANK, "bank%d" % (3 - n), False)
+                gather(a_at1[:, r, :], a[r], idx1[:])
+                nc.vector.tensor_copy(f1[r % 2][:].indirect(idx2[:]), a_at1[:, r, :])
+            nc.gpsimd.tensor_tensor(c1[r][:], a[r][:], f1[r % 2][:], ALU.subtract)
+
+        scaled6 = [None] * PACK
+
+        def scale_at6(r, tag=None):
+            scaled6[r] = sb("scaled6_%d" % r, [P, I], F32, tag=tag)
+            nc.scalar.activation(scaled6[r][:], c1_at6[:, r, :], COPY, scale=row_factor[:, r : r + 1])
+
+        def finish(r, cols):
+            nc.vector.scalar_tensor_tensor(
+                out=gw[:, r, cols],
+                in0=c2_at5[:, r, cols],
+                scalar=row_factor[:, r : r + 1],
+                in1=scaled6[r][:, cols],
+                op0=ALU.mult,
+                op1=ALU.subtract,
+            )
+
+        for r in range(PACK):
+            gather(c1_at3[:, r, :], c1[r], idx3[:])
+        for r in range(PACK):
+            gather(c1_at6[:, r, :], c1[r], idx6[:])
+            if r > 1:
+                scale_at6(r)
+
+        for r in range(PACK):
+            if r % 2 == 0:
+                nc.vector.tensor_tensor(w[:, r : r + 2, :], c1_at3[:, r : r + 2, :], a_at1[:, r : r + 2, :], ALU.max)
+            nc.vector.tensor_copy(f2[r % 2][:].indirect(idx4[:]), w[:, r, :])
+            if r < PACK - 1:
+                nc.gpsimd.tensor_tensor(c2[r][:], c1[r][:], f2[r % 2][:], ALU.add)
+                gather(c2_at5[:, r, :], c2[r], idx5[:])
+            else:
+                nc.vector.tensor_tensor(c2[r][:], c1[r][:], f2[r % 2][:], ALU.add)
+            if r == 1:
+                g0 = sb("g0", [P, I], F32)
+                nc.gpsimd.tensor_tensor(g0[:], c2_at5[:, 0, :], c1_at6[:, 0, :], ALU.subtract)
+                nc.scalar.activation(gw[:, 0, :], g0[:], COPY, scale=row_factor[:, 0:1])
+        last = PACK - 1
+        for h in range(2):
+            gather(c2_at5[:, last, half(h)], c2[last], half_list(idx5, h))
+        scale_at6(1, tag="c1_2")
+        finish(2, slice(0, I))
+        finish(1, slice(0, I))
+        for h in range(2):
+            finish(last, half(h))
+
+        gw_words = sb("gw_words", [P, I, PACK], BF16)
+        g_codes = sb("g_codes", [P, I], U32)
+        g_scales = sb("g_scales", [P, I], U8)
+
+        def weave(cols):
+            dst = gw_words[:, cols, :].rearrange("p (c i) r -> p c r i", i=4)
+            return dst, gw[:, :, cols].rearrange("p r (c i) -> p c r i", i=4)
+
+        nc.vector.tensor_copy(*weave(half(0)))
+        nc.vector.tensor_copy(*weave(slice(HALF, HALF + HALF // 2)))
+        nc.scalar.copy(*weave(slice(HALF + HALF // 2, I)))
+        words_flat = gw_words[:].rearrange("p i r -> p (i r)")
+        for h in range(2):
+            nc.vector.quantize_mx(
+                out=g_codes[:, half(h)].bitcast(FP8X4),
+                scales=g_scales[:, half(h)],
+                in_=words_flat[:, h * HALF * PACK : (h + 1) * HALF * PACK],
+            )
+
+        def mix(dst, b, h):
+            nc.tensor.matmul_mx(
+                out=dst,
+                lhsT=m_words[:, b * P : (b + 1) * P].bitcast(FP8X4),
+                lhsT_scale=m_scales[:, b * P : (b + 1) * P],
+                rhs=g_codes[:, half(h)].bitcast(FP8X4),
+                rhs_scale=g_scales[:, half(h)],
+                start=True,
+                stop=True,
+            )
+
+        out_blocks = out.rearrange("(b p) i -> p b i", p=P)
+        first_bank = psum.tile([P, 2, HALF], F32, name="first_bank")
+        first = sb("first", [P, 2, HALF], F32)
+        for b in range(2):
+            mix(first_bank[:, b, :], b, 0)
+        nc.scalar.activation(first[:], first_bank[:], COPY)
+        nc.sync.dma_start(out=out_blocks[:, :, half(0)], in_=first[:])
+        for b in range(2):
+            second_bank = psum.tile([P, HALF], F32, name="second_bank%d" % b)
+            second = sb("second%d" % b, [P, HALF], F32)
+            mix(second_bank[:], b, 1)
+            if b == 0:
+                nc.vector.tensor_copy(out=second[:], in_=second_bank[:])
+                nc.sync.dma_start(out=out_blocks[:, b, half(1)], in_=second[:])
+            else:
+                nc.scalar.activation(second[:], second_bank[:], COPY)
+                nc.scalar.dma_start(out=out_blocks[:, b, half(1)], in_=second[:])

@@ -21,6 +21,7 @@ PACK = 4
 BANK = 512
 HALF = I // 2
 LIST_COLS = I // 16
+OVERHANG = 16
 
 
 def tile_attend_backtrack_one_mixed_kernel(
@@ -88,10 +89,8 @@ def tile_attend_backtrack_one_mixed_kernel(
         q_flat = q_bf[:].rearrange("p r m j -> p (r m j)")
 
         def deal_queries(h, r0, r1):
-            nc.vector.tensor_copy(
-                out=q_bf[:, r0:r1, h * P // 2 : (h + 1) * P // 2, :].rearrange("p r m j -> p m j r"),
-                in_=q_raw[h][:].rearrange("p j (m r) -> p m j r", r=PACK)[:, :, :, r0:r1],
-            )
+            dst = q_bf[:, r0:r1, h * P // 2 : (h + 1) * P // 2, :].rearrange("p r m j -> p m j r")
+            return dst, q_raw[h][:].rearrange("p j (m r) -> p m j r", r=PACK)[:, :, :, r0:r1]
 
         def quantize_queries(r0, r1):
             nc.vector.quantize_mx(
@@ -100,18 +99,18 @@ def tile_attend_backtrack_one_mixed_kernel(
                 in_=q_flat[:, r0 * P * PACK : r1 * P * PACK],
             )
 
-        deal_queries(0, 0, PACK)
-        deal_queries(1, 0, 1)
+        for h in range(2):
+            nc.vector.tensor_copy(*deal_queries(h, 0, 1))
+            nc.scalar.activation(*deal_queries(h, 1, PACK), COPY)
         quantize_queries(0, 1)
 
         a = [sb("a%d" % r, [P, T], F32) for r in range(PACK)]
         c1 = [sb("c1_%d" % r, [P, T], F32) for r in range(PACK)]
-        c2 = [sb("c2_%d" % r, [P, T], F32) for r in range(PACK)]
         a_at1 = sb("a_at1", [P, PACK, I], F32)
         c1_at3 = sb("c1_at3", [P, PACK, I], F32)
         w = sb("w", [P, PACK, I], F32)
-        c1_at6 = sb("c1_at6", [P, PACK, I], F32)
-        c2_at5 = sb("c2_at5", [P, PACK, I], F32)
+        c1_at6 = [sb("c1_at6_%d" % r, [P, I], F32) for r in range(PACK)]
+        c2_at5 = [None] * PACK
         gw = sb("gw", [P, PACK, I], BF16)
 
         def gather(dst, window, offsets):
@@ -138,7 +137,6 @@ def tile_attend_backtrack_one_mixed_kernel(
             if r == 0:
                 for n in range(4):
                     scores(r, n, T // 4, "bank%d" % n, n % 2 == 0)
-                deal_queries(1, 1, PACK)
                 quantize_queries(1, 2)
                 quantize_queries(2, PACK)
                 for h in range(2):
@@ -155,12 +153,12 @@ def tile_attend_backtrack_one_mixed_kernel(
 
         def scale_at6(r, tag=None):
             scaled6[r] = sb("scaled6_%d" % r, [P, I], F32, tag=tag)
-            nc.scalar.activation(scaled6[r][:], c1_at6[:, r, :], COPY, scale=row_factor[:, r : r + 1])
+            nc.scalar.activation(scaled6[r][:], c1_at6[r][:], COPY, scale=row_factor[:, r : r + 1])
 
         def finish(r, cols):
             nc.vector.scalar_tensor_tensor(
                 out=gw[:, r, cols],
-                in0=c2_at5[:, r, cols],
+                in0=c2_at5[r][:, cols],
                 scalar=row_factor[:, r : r + 1],
                 in1=scaled6[r][:, cols],
                 op0=ALU.mult,
@@ -170,29 +168,37 @@ def tile_attend_backtrack_one_mixed_kernel(
         for r in range(PACK):
             gather(c1_at3[:, r, :], c1[r], idx3[:])
         for r in range(PACK):
-            gather(c1_at6[:, r, :], c1[r], idx6[:])
+            gather(c1_at6[r][:], c1[r], idx6[:])
             if r > 1:
                 scale_at6(r)
 
+        def larger(cols):
+            flat = [x[:].rearrange("p r i -> p (r i)")[:, cols] for x in (w, c1_at3, a_at1)]
+            nc.vector.tensor_tensor(*flat, ALU.max)
+
+        last = PACK - 1
         for r in range(PACK):
             if r % 2 == 0:
-                nc.vector.tensor_tensor(w[:, r : r + 2, :], c1_at3[:, r : r + 2, :], a_at1[:, r : r + 2, :], ALU.max)
+                larger(slice(r * I, (r + 1) * I + OVERHANG))
+                larger(slice((r + 1) * I + OVERHANG, (r + 2) * I))
             nc.vector.tensor_copy(f2[r % 2][:].indirect(idx4[:]), w[:, r, :])
-            if r < PACK - 1:
-                nc.gpsimd.tensor_tensor(c2[r][:], c1[r][:], f2[r % 2][:], ALU.add)
-                gather(c2_at5[:, r, :], c2[r], idx5[:])
+            c2 = sb("c2_%d" % r, [P, T], F32, tag="c1_at6_0" if r == 2 else None)
+            if r < last:
+                nc.gpsimd.tensor_tensor(c2[:], c1[r][:], f2[r % 2][:], ALU.add)
+                c2_at5[r] = sb("c2_at5_%d" % r, [P, I], F32)
+                gather(c2_at5[r][:], c2, idx5[:])
             else:
-                nc.vector.tensor_tensor(c2[r][:], c1[r][:], f2[r % 2][:], ALU.add)
+                nc.vector.tensor_tensor(c2[:], c1[r][:], f2[r % 2][:], ALU.add)
+                c2_at5[r] = sb("c2_at5_%d" % r, [P, I], F32, tag="c1_2")
+                for h in range(2):
+                    gather(c2_at5[r][:, half(h)], c2, half_list(idx5, h))
             if r == 1:
                 g0 = sb("g0", [P, I], F32)
-                nc.gpsimd.tensor_tensor(g0[:], c2_at5[:, 0, :], c1_at6[:, 0, :], ALU.subtract)
+                nc.gpsimd.tensor_tensor(g0[:], c2_at5[0][:], c1_at6[0][:], ALU.subtract)
+                scale_at6(1, tag="c2_at5_0")
                 nc.scalar.activation(gw[:, 0, :], g0[:], COPY, scale=row_factor[:, 0:1])
-        last = PACK - 1
-        for h in range(2):
-            gather(c2_at5[:, last, half(h)], c2[last], half_list(idx5, h))
-        scale_at6(1, tag="c1_2")
-        finish(2, slice(0, I))
         finish(1, slice(0, I))
+        finish(2, slice(0, I))
         for h in range(2):
             finish(last, half(h))
 
@@ -204,9 +210,11 @@ def tile_attend_backtrack_one_mixed_kernel(
             dst = gw_words[:, cols, :].rearrange("p (c i) r -> p c r i", i=4)
             return dst, gw[:, :, cols].rearrange("p r (c i) -> p c r i", i=4)
 
-        nc.vector.tensor_copy(*weave(half(0)))
-        nc.vector.tensor_copy(*weave(slice(HALF, HALF + HALF // 2)))
-        nc.scalar.copy(*weave(slice(HALF + HALF // 2, I)))
+        quarter = [slice(n * I // 4, (n + 1) * I // 4) for n in range(4)]
+        nc.scalar.copy(*weave(quarter[0]))
+        nc.vector.tensor_copy(*weave(quarter[1]))
+        nc.vector.tensor_copy(*weave(quarter[2]))
+        nc.scalar.copy(*weave(quarter[3]))
         words_flat = gw_words[:].rearrange("p i r -> p (i r)")
         for h in range(2):
             nc.vector.quantize_mx(
@@ -215,31 +223,22 @@ def tile_attend_backtrack_one_mixed_kernel(
                 in_=words_flat[:, h * HALF * PACK : (h + 1) * HALF * PACK],
             )
 
-        def mix(dst, b, h):
-            nc.tensor.matmul_mx(
-                out=dst,
-                lhsT=m_words[:, b * P : (b + 1) * P].bitcast(FP8X4),
-                lhsT_scale=m_scales[:, b * P : (b + 1) * P],
-                rhs=g_codes[:, half(h)].bitcast(FP8X4),
-                rhs_scale=g_scales[:, half(h)],
-                start=True,
-                stop=True,
-            )
-
-        out_blocks = out.rearrange("(b p) i -> p b i", p=P)
-        first_bank = psum.tile([P, 2, HALF], F32, name="first_bank")
-        first = sb("first", [P, 2, HALF], F32)
-        for b in range(2):
-            mix(first_bank[:, b, :], b, 0)
-        nc.scalar.activation(first[:], first_bank[:], COPY)
-        nc.sync.dma_start(out=out_blocks[:, :, half(0)], in_=first[:])
-        for b in range(2):
-            second_bank = psum.tile([P, HALF], F32, name="second_bank%d" % b)
-            second = sb("second%d" % b, [P, HALF], F32)
-            mix(second_bank[:], b, 1)
-            if b == 0:
-                nc.vector.tensor_copy(out=second[:], in_=second_bank[:])
-                nc.sync.dma_start(out=out_blocks[:, b, half(1)], in_=second[:])
-            else:
-                nc.scalar.activation(second[:], second_bank[:], COPY)
-                nc.scalar.dma_start(out=out_blocks[:, b, half(1)], in_=second[:])
+        for h in range(2):
+            for b in range(E // P):
+                bank = psum.tile([P, HALF], F32, name="mix_bank%d%d" % (h, b))
+                nc.tensor.matmul_mx(
+                    out=bank[:],
+                    lhsT=m_words[:, b * P : (b + 1) * P].bitcast(FP8X4),
+                    lhsT_scale=m_scales[:, b * P : (b + 1) * P],
+                    rhs=g_codes[:, half(h)].bitcast(FP8X4),
+                    rhs_scale=g_scales[:, half(h)],
+                    start=True,
+                    stop=True,
+                )
+                result = sb("result%d%d" % (h, b), [P, HALF], F32)
+                if b == 0:
+                    nc.scalar.activation(result[:], bank[:], COPY)
+                else:
+                    nc.vector.tensor_copy(out=result[:], in_=bank[:])
+                queue = nc.scalar if (h, b) == (1, 1) else nc.sync
+                queue.dma_start(out=out[b * P : (b + 1) * P, half(h)], in_=result[:])

from contextlib import ExitStack

import concourse.mybir as mybir

D, T, I, Q, E = 512, 1024, 512, 512, 256
FLOPS = 2 * D * Q * T + 2 * Q * E * I

F32 = mybir.dt.float32
BF16 = mybir.dt.bfloat16
I32 = mybir.dt.int32
U32 = mybir.dt.uint32
U16 = mybir.dt.uint16
U8 = mybir.dt.uint8
FP8X4 = mybir.dt.float8_e4m3fn_x4
FP4X4 = mybir.dt.float4_e2m1fn_x4
ALU = mybir.AluOpType
COPY = mybir.ActivationFunctionType.Copy

P = 128
PACK = 4
BANK = 512
HALF = I // 2
LIST_COLS = I // 16
OVERHANG = 16


def tile_attend_backtrack_one_mixed_kernel(
    tc, query, keys_words, keys_scales, rowf, mix_words, mix_scales, offs, offs2, offs3, offs4, offs5, offs6, out
):
    nc = tc.nc
    with ExitStack() as ctx:
        lists = ctx.enter_context(tc.tile_pool(name="lists", bufs=1))
        keep = ctx.enter_context(tc.tile_pool(name="keep", bufs=1))
        psum = ctx.enter_context(tc.psum_pool(name="psum", bufs=1))

        def sb(name, shape, dtype, tag=None):
            return keep.tile(shape, dtype, name=name, tag=tag or name, align_bytes=64)

        idx1 = lists.tile([P, LIST_COLS], U16, name="idx1")
        idx2 = lists.tile([P, LIST_COLS], U16, name="idx2")
        idx3 = lists.tile([P, LIST_COLS], U16, name="idx3")
        idx4 = lists.tile([P, LIST_COLS], U16, name="idx4")
        idx5 = lists.tile([P, LIST_COLS], U16, name="idx5")
        idx6 = lists.tile([P, LIST_COLS], U16, name="idx6")

        def half_list(idx, h):
            return idx[:, h * LIST_COLS // 2 : (h + 1) * LIST_COLS // 2]

        def half(h):
            return slice(h * HALF, (h + 1) * HALF)

        k_words = sb("k_words", [P, 2 * T], U8)
        k_scales = sb("k_scales", [P, T], U8)
        m_words = sb("m_words", [P, E], U32)
        m_scales = sb("m_scales", [P, E], U8)
        row_factor = sb("row_factor", [P, PACK], F32)
        q_raw = [sb("q_raw%d" % h, [P, PACK, Q // 2], F32) for h in range(2)]
        f1 = [sb("f1_%d" % b, [P, T], F32) for b in range(2)]
        f2 = [sb("f2_%d" % b, [P, T], F32) for b in range(2)]

        nc.vector.memset(k_scales[:].bitcast(U32), 0)
        q_rows = query.rearrange("(p j) q -> p j q", j=PACK)
        nc.sync.dma_start(out=q_raw[0][:], in_=q_rows[:, :, 0 : Q // 2])
        for g in range(4):
            nc.sync.dma_start(
                out=k_scales[32 * g : 32 * g + 4, :].bitcast(I32), in_=keys_scales[0, 4 * g : 4 * g + 4, :].bitcast(I32)
            )
        nc.sync.dma_start(out=q_raw[1][:], in_=q_rows[:, :, Q // 2 : Q])
        nc.sync.dma_start(out=k_words[:].bitcast(I32), in_=keys_words[0].bitcast(I32))
        nc.sync.dma_start(idx1[:], offs)
        nc.sync.dma_start(idx2[:], offs2)
        nc.sync.dma_start(idx3[:], offs3)
        nc.sync.dma_start(idx6[:], offs6)
        nc.sync.dma_start(out=row_factor[:], in_=rowf.rearrange("(p r) o -> p (r o)", r=PACK))
        nc.sync.dma_start(idx4[:], offs4)
        nc.sync.dma_start(idx5[:], offs5)
        for window in f1 + f2:
            nc.vector.memset(window[:], 0.0)
        nc.vector.memset(m_scales[:].bitcast(U32), 0)
        nc.sync.dma_start(out=m_words[:].bitcast(I32), in_=mix_words[0].rearrange("p n t -> p (n t)").bitcast(I32))
        for g in range(4):
            nc.sync.dma_start(
                out=m_scales[32 * g : 32 * g + 4, :].bitcast(I32), in_=mix_scales[0, 4 * g : 4 * g + 4, :].bitcast(I32)
            )

        q_bf = sb("q_bf", [P, PACK, P, PACK], BF16)
        q_codes = sb("q_codes", [P, Q], U32)
        q_scales = sb("q_scales", [P, Q], U8)
        q_flat = q_bf[:].rearrange("p r m j -> p (r m j)")

        def deal_queries(h, r0, r1):
            dst = q_bf[:, r0:r1, h * P // 2 : (h + 1) * P // 2, :].rearrange("p r m j -> p m j r")
            return dst, q_raw[h][:].rearrange("p j (m r) -> p m j r", r=PACK)[:, :, :, r0:r1]

        def quantize_queries(r0, r1):
            nc.vector.quantize_mx(
                out=q_codes[:, r0 * P : r1 * P].bitcast(FP8X4),
                scales=q_scales[:, r0 * P : r1 * P],
                in_=q_flat[:, r0 * P * PACK : r1 * P * PACK],
            )

        for h in range(2):
            nc.vector.tensor_copy(*deal_queries(h, 0, 1))
            nc.scalar.activation(*deal_queries(h, 1, PACK), COPY)
        quantize_queries(0, 1)

        a = [sb("a%d" % r, [P, T], F32) for r in range(PACK)]
        c1 = [sb("c1_%d" % r, [P, T], F32) for r in range(PACK)]
        a_at1 = sb("a_at1", [P, PACK, I], F32)
        c1_at3 = sb("c1_at3", [P, PACK, I], F32)
        w = sb("w", [P, PACK, I], F32)
        c1_at6 = [sb("c1_at6_%d" % r, [P, I], F32) for r in range(PACK)]
        c2_at5 = [None] * PACK
        gw = sb("gw", [P, PACK, I], BF16)

        def gather(dst, window, offsets):
            nc.scalar.activation(dst, window[:].indirect(offsets), COPY)

        def scores(r, n, width, bank_tag, on_vector):
            cols = slice(n * width, (n + 1) * width)
            bank = psum.tile([P, width], F32, name="score_bank", tag=bank_tag)
            nc.tensor.matmul_mx(
                out=bank[:],
                lhsT=q_codes[:, r * P : (r + 1) * P].bitcast(FP8X4),
                lhsT_scale=q_scales[:, r * P : (r + 1) * P],
                rhs=k_words[:, 2 * n * width : 2 * (n + 1) * width].bitcast(FP4X4),
                rhs_scale=k_scales[:, cols],
                start=True,
                stop=True,
            )
            if on_vector:
                nc.vector.tensor_copy(out=a[r][:, cols], in_=bank[:])
            else:
                nc.scalar.activation(a[r][:, cols], bank[:], COPY)

        for r in range(PACK):
            if r == 0:
                for n in range(4):
                    scores(r, n, T // 4, "bank%d" % n, n % 2 == 0)
                quantize_queries(1, 2)
                quantize_queries(2, PACK)
                for h in range(2):
                    gather(a_at1[:, r, half(h)], a[r], half_list(idx1, h))
                    nc.vector.tensor_copy(f1[r % 2][:].indirect(half_list(idx2, h)), a_at1[:, r, half(h)])
            else:
                for n in range(2):
                    scores(r, n, BANK, "bank%d" % (3 - n), False)
                gather(a_at1[:, r, :], a[r], idx1[:])
                nc.vector.tensor_copy(f1[r % 2][:].indirect(idx2[:]), a_at1[:, r, :])
            nc.gpsimd.tensor_tensor(c1[r][:], a[r][:], f1[r % 2][:], ALU.subtract)

        scaled6 = [None] * PACK

        def scale_at6(r, tag=None):
            scaled6[r] = sb("scaled6_%d" % r, [P, I], F32, tag=tag)
            nc.scalar.activation(scaled6[r][:], c1_at6[r][:], COPY, scale=row_factor[:, r : r + 1])

        def finish(r, cols):
            nc.vector.scalar_tensor_tensor(
                out=gw[:, r, cols],
                in0=c2_at5[r][:, cols],
                scalar=row_factor[:, r : r + 1],
                in1=scaled6[r][:, cols],
                op0=ALU.mult,
                op1=ALU.subtract,
            )

        for r in range(PACK):
            gather(c1_at3[:, r, :], c1[r], idx3[:])
        for r in range(PACK):
            gather(c1_at6[r][:], c1[r], idx6[:])
            if r > 1:
                scale_at6(r)

        def larger(cols):
            flat = [x[:].rearrange("p r i -> p (r i)")[:, cols] for x in (w, c1_at3, a_at1)]
            nc.vector.tensor_tensor(*flat, ALU.max)

        last = PACK - 1
        for r in range(PACK):
            if r % 2 == 0:
                larger(slice(r * I, (r + 1) * I + OVERHANG))
                larger(slice((r + 1) * I + OVERHANG, (r + 2) * I))
            nc.vector.tensor_copy(f2[r % 2][:].indirect(idx4[:]), w[:, r, :])
            c2 = sb("c2_%d" % r, [P, T], F32, tag="c1_at6_0" if r == 2 else None)
            if r < last:
                nc.gpsimd.tensor_tensor(c2[:], c1[r][:], f2[r % 2][:], ALU.add)
                c2_at5[r] = sb("c2_at5_%d" % r, [P, I], F32)
                gather(c2_at5[r][:], c2, idx5[:])
            else:
                nc.vector.tensor_tensor(c2[:], c1[r][:], f2[r % 2][:], ALU.add)
                c2_at5[r] = sb("c2_at5_%d" % r, [P, I], F32, tag="c1_2")
                for h in range(2):
                    gather(c2_at5[r][:, half(h)], c2, half_list(idx5, h))
            if r == 1:
                g0 = sb("g0", [P, I], F32)
                nc.gpsimd.tensor_tensor(g0[:], c2_at5[0][:], c1_at6[0][:], ALU.subtract)
                scale_at6(1, tag="c2_at5_0")
                nc.scalar.activation(gw[:, 0, :], g0[:], COPY, scale=row_factor[:, 0:1])
        finish(1, slice(0, I))
        finish(2, slice(0, I))
        for h in range(2):
            finish(last, half(h))

        gw_words = sb("gw_words", [P, I, PACK], BF16)
        g_codes = sb("g_codes", [P, I], U32)
        g_scales = sb("g_scales", [P, I], U8)

        def weave(cols):
            dst = gw_words[:, cols, :].rearrange("p (c i) r -> p c r i", i=4)
            return dst, gw[:, :, cols].rearrange("p r (c i) -> p c r i", i=4)

        quarter = [slice(n * I // 4, (n + 1) * I // 4) for n in range(4)]
        nc.scalar.copy(*weave(quarter[0]))
        nc.vector.tensor_copy(*weave(quarter[1]))
        nc.vector.tensor_copy(*weave(quarter[2]))
        nc.scalar.copy(*weave(quarter[3]))
        words_flat = gw_words[:].rearrange("p i r -> p (i r)")
        for h in range(2):
            nc.vector.quantize_mx(
                out=g_codes[:, half(h)].bitcast(FP8X4),
                scales=g_scales[:, half(h)],
                in_=words_flat[:, h * HALF * PACK : (h + 1) * HALF * PACK],
            )

        for h in range(2):
            for b in range(E // P):
                bank = psum.tile([P, HALF], F32, name="mix_bank%d%d" % (h, b))
                nc.tensor.matmul_mx(
                    out=bank[:],
                    lhsT=m_words[:, b * P : (b + 1) * P].bitcast(FP8X4),
                    lhsT_scale=m_scales[:, b * P : (b + 1) * P],
                    rhs=g_codes[:, half(h)].bitcast(FP8X4),
                    rhs_scale=g_scales[:, half(h)],
                    start=True,
                    stop=True,
                )
                result = sb("result%d%d" % (h, b), [P, HALF], F32)
                if b == 0:
                    nc.scalar.activation(result[:], bank[:], COPY)
                else:
                    nc.vector.tensor_copy(out=result[:], in_=bank[:])
                queue = nc.scalar if (h, b) == (1, 1) else nc.sync
                queue.dma_start(out=out[b * P : (b + 1) * P, half(h)], in_=result[:])
